import numpy as np
import ml_dtypes


def mxq(x, axis, fmt="e4m3"):
    dtype, down = {"e4m3": (ml_dtypes.float8_e4m3fn, 7), "e5m2": (ml_dtypes.float8_e5m2, 14)}[fmt]
    v = np.moveaxis(np.asarray(x, np.float32).astype(ml_dtypes.bfloat16).astype(np.float64), axis, -1)
    blocks = v.reshape(v.shape[:-1] + (-1, 32))
    amax = np.abs(blocks).max(-1, keepdims=True)
    byte = np.maximum(np.where(amax > 0, np.frexp(amax)[1] - 1 + 127, 0) - down, 1)
    scale = np.exp2(byte - 127.0)
    codes = (blocks / scale).astype(np.float32).astype(dtype).astype(np.float64)
    return np.moveaxis((codes * scale).reshape(v.shape), -1, axis)


WIDE = False


def mx_kscale(k):
    if not WIDE:
        return np.ones(k)
    levels = np.array([10, -10, 5, -5, 0])
    if k % 512:
        return np.exp2(np.random.permutation(np.resize(levels, k // 32))).repeat(32)
    a = np.empty((k // 512, 16))
    for p in range(k // 512):
        a[p, :8] = np.random.permutation(np.resize(levels, 8))
        for g in range(8):
            far = levels[np.abs(levels - a[p, g]) >= 10]
            a[p, g + 8] = far[np.random.randint(len(far))]
    return np.exp2(a.ravel()).repeat(32)


def f64(x):
    return np.asarray(x).astype(np.float64)


def striped(idx):
    return np.tile(np.asarray(idx).reshape(-1, 16).T, (8, 1)).astype(np.uint16)


def unstriped(offs):
    return offs[:16].T.reshape(-1).astype(np.int64)


E2M1 = np.array([0.0, 0.5, 1.0, 1.5, 2.0, 3.0, 4.0, 6.0, -0.0, -0.5, -1.0, -1.5, -2.0, -3.0, -4.0, -6.0])


def pack_weight(w, fmt):
    k, n = w.shape
    w = f64(np.asarray(w, np.float32).astype(ml_dtypes.bfloat16)).reshape(k // 32, 32, n)
    amax = np.abs(w).max(1)
    if fmt == "e4m3":
        byte = np.frexp(amax)[1] - 1 + 127 - 7
    else:
        mant, ex = np.frexp(amax / 6.0)
        byte = np.where(mant > 0.5, ex, ex - 1) + 127
    byte = np.clip(np.where(amax > 0, byte, 1), 1, 254)
    scaled = (w * np.exp2(127.0 - byte)[:, None, :]).reshape(k, n).astype(np.float32)
    by_word = np.ascontiguousarray(scaled.reshape(k // 512, 128, 4, n).transpose(0, 1, 3, 2))
    if fmt == "e4m3":
        words = by_word.astype(ml_dtypes.float8_e4m3fn).view(np.uint8)
    else:
        c = by_word.astype(ml_dtypes.float4_e2m1fn).view(np.uint8) & 0xF
        words = (c[..., 0::2] | (c[..., 1::2] << 4)).reshape(k // 512, 128, 2 * n)
    return np.ascontiguousarray(words), np.ascontiguousarray(byte.astype(np.uint8).reshape(k // 512, 16, n))


def unpack_weight(words, scales, fmt):
    g, _, n = scales.shape
    words = np.ascontiguousarray(words).reshape(g, 128, n, -1)
    if fmt == "e4m3":
        vals = words.view(ml_dtypes.float8_e4m3fn).astype(np.float64)
    else:
        nib = np.empty((g, 128, n, 4), np.uint8)
        nib[..., 0::2] = words & 0xF
        nib[..., 1::2] = words >> 4
        vals = E2M1[nib]
    vals = vals * np.repeat(np.exp2(scales.astype(np.float64) - 127.0), 8, axis=1)[..., None]
    return vals.transpose(0, 1, 3, 2).reshape(g * 512, n)


D, T, I, Q, E, N, M = 512, 2048, 512, 256, 512, 64, 1024


def setup_inputs():
    n = np.random.standard_normal
    idx = np.random.permutation(T)[:I]
    idx2 = np.random.permutation(M)[:Q]
    fd = mx_kscale(D)
    fi = mx_kscale(I)
    ti = np.ones(T)
    ti[idx] = fi
    keysp = pack_weight(n((D, T)) / fd[:, None], "e4m3")
    return {
        "query": (n((D, Q)) * 0.9 / np.sqrt(D) * fd[:, None]).astype(np.float32),
        "keys_words": keysp[0],
        "keys_scales": keysp[1],
        "lam": (np.random.uniform(0.4, 0.9, (Q, 1))).astype(np.float32),
        "reserve": (np.random.uniform(0.5, 2.0, (Q, 1))).astype(np.float32),
        "os": (np.random.uniform(4.0, 16.0, (1, I)) * fi).astype(np.float32),
        "vals": (n((E, T)) / ti).astype(np.float32),
        "old": (n((E, M)) * 2.0).astype(np.float32),
        "fade": (np.random.uniform(0.3, 0.9, (1, M))).astype(np.float32),
        "offs": striped(idx),
        "offs2": striped(idx2),
    }


def reference(query, keys_words, keys_scales, lam, reserve, os, vals, old, fade, offs, offs2):
    idx = unstriped(offs)
    idx2 = unstriped(offs2)
    keysu = unpack_weight(keys_words, keys_scales, "e4m3")
    queryq = mxq(f64(query), 0, "e4m3")
    keysidxg = keysu[:, idx]
    a = queryq.T @ keysidxg
    mb = a.reshape(Q, N, I // N).max(axis=2)
    mr = np.repeat(mb, I // N, axis=1)
    s = a - mr * f64(lam)
    p = np.exp(s - np.max(s, axis=1, keepdims=True))
    r = p / np.sum(p, axis=1, keepdims=True)
    u0 = r * np.log(r) * (-1.0)
    w = u0 / (np.sum(u0, axis=1, keepdims=True) + f64(reserve))
    wo1 = w * f64(os)
    wt1 = wo1.T
    vt1 = f64(vals)[:, idx].T
    vt1q = mxq(vt1, 0, "e4m3")
    wt1q = mxq(wt1, 0, "e4m3")
    o = vt1q.T @ wt1q
    of = np.zeros((E, M))
    of[:, idx2] = o
    y = f64(old) * f64(fade) + of
    return y

@@ -1,0 +1,276 @@
+from contextlib import ExitStack
+
+import concourse.mybir as mybir
+from concourse.masks import make_identity
+
+D, T, I, Q, E, M = 512, 2048, 512, 256, 512, 1024
+PAGE = 8
+P = 128
+PACK = 4
+FLOPS = 2 * D * Q * I + 2 * I * E * Q
+
+F32 = mybir.dt.float32
+BF16 = mybir.dt.bfloat16
+I32 = mybir.dt.int32
+U32 = mybir.dt.uint32
+U16 = mybir.dt.uint16
+U8 = mybir.dt.uint8
+FP8X4 = mybir.dt.float8_e4m3fn_x4
+ALU = mybir.AluOpType
+ACT = mybir.ActivationFunctionType
+AX = mybir.AxisListType
+
+Q_TILES = Q // P
+E_TILES = E // P
+BANK = 512
+M_BANKS = M // BANK
+PAGES = I // PAGE
+WIDE = I + 8
+
+
+def tile_attend_pagegap_lacking_written_kernel(
+    tc, query, keys_words, keys_scales, lam, reserve, slot_factor, vals, old, fade, offs, offs2, out
+):
+    nc = tc.nc
+    with ExitStack() as ctx:
+        lists = ctx.enter_context(tc.tile_pool(name="lists", bufs=1))
+        sb = ctx.enter_context(tc.tile_pool(name="sb", bufs=1))
+        ps = ctx.enter_context(tc.psum_pool(name="ps", bufs=1))
+
+        def bank(tag, name):
+            return ps.tile([P, BANK], F32, tag=tag, name=name)
+
+        key_scale_pool = sb.tile([P, T], U8, align_bytes=64)
+
+        slot_list = lists.tile([P, I // 16], U16)
+        nc.sync.dma_start(slot_list[:], offs)
+        for quad in range(4):
+            nc.sync.dma_start(
+                key_scale_pool[32 * quad : 32 * quad + 32, :].bitcast(I32),
+                keys_scales[0, 4 * quad : 4 * quad + 4, :].bitcast(I32).partition_broadcast(8),
+            )
+        query_raw = sb.tile([P, PACK, Q], F32)
+        nc.sync.dma_start(query_raw[:], query.rearrange("(p t) q -> p t q", t=PACK))
+        key_pool = sb.tile([P, T], I32, align_bytes=64)
+        nc.sync.dma_start(key_pool[:], keys_words[0].rearrange("p c t -> p (c t)").bitcast(I32))
+
+        lam_col = sb.tile([P, Q_TILES], F32)
+        reserve_col = sb.tile([P, Q_TILES], F32)
+        os_col = sb.tile([P, PACK], F32)
+        fade_col = sb.tile([P, M_BANKS, PACK], F32)
+        identity = sb.tile([P, P], F32)
+        with nc.allow_non_contiguous_dma(reason="one value a query row"):
+            nc.sync.dma_start(lam_col[:], lam.rearrange("(h p) o -> p (h o)", p=P))
+        make_identity(nc, identity[:])
+
+        val_pool = [sb.tile([P, T], F32, name=f"val_pool{j}", tag=f"val_pool{j}") for j in range(E_TILES)]
+        old_sb = [sb.tile([P, M], F32, name=f"old_sb{j}", tag=f"old_sb{j}", align_bytes=64) for j in range(E_TILES)]
+        place_list = lists.tile([P, Q // 16], U16)
+        nc.sync.dma_start(val_pool[0][:], vals[0:P, :])
+        nc.sync.dma_start(fade_col[:], fade.rearrange("o (h p t) -> p (o h) t", p=P, t=PACK))
+        nc.sync.dma_start(old_sb[0][:], old[0:P, :])
+        nc.sync.dma_start(old_sb[1][:], old[P : 2 * P, :])
+        nc.sync.dma_start(val_pool[1][:], vals[P : 2 * P, :])
+        with nc.allow_non_contiguous_dma(reason="one value a query row"):
+            nc.sync.dma_start(reserve_col[:], reserve.rearrange("(h p) o -> p (h o)", p=P))
+        nc.sync.dma_start(val_pool[2][:], vals[2 * P : 3 * P, :])
+        nc.sync.dma_start(os_col[:], slot_factor.rearrange("o (p t) -> p (o t)", t=PACK))
+        nc.sync.dma_start(place_list[:], offs2)
+        nc.sync.dma_start(val_pool[3][:], vals[3 * P : 4 * P, :])
+        for j in range(2, E_TILES):
+            nc.sync.dma_start(old_sb[j][:], old[j * P : (j + 1) * P, :])
+
+        placed = [sb.tile([P, M], F32, name=f"placed{j}") for j in range(E_TILES)]
+        for j in range(E_TILES):
+            nc.vector.memset(placed[j][:], 0.0)
+
+        key_scales = sb.tile([P, I], U8, align_bytes=64)
+        nc.vector.tensor_copy(key_scales[:], key_scale_pool[:].indirect(slot_list[:]))
+        query_bf = sb.tile([P, Q, PACK], BF16, align_bytes=64)
+        nc.scalar.copy(
+            query_bf[:].rearrange("p (c n) t -> p c t n", n=4),
+            query_raw[:].rearrange("p t (c n) -> p c t n", n=4),
+        )
+        query_codes = sb.tile([P, Q], U32, align_bytes=64)
+        query_scales = sb.tile([P, Q], U8, align_bytes=64)
+        nc.vector.quantize_mx(
+            out=query_codes[:].bitcast(FP8X4), scales=query_scales[:], in_=query_bf[:].rearrange("p q t -> p (q t)")
+        )
+        key_codes = sb.tile([P, I], U32, align_bytes=64)
+        nc.vector.tensor_copy(key_codes[:], key_pool[:].bitcast(U32).indirect(slot_list[:]))
+
+        minus_lam = sb.tile([P, Q_TILES], F32)
+        nc.gpsimd.tensor_scalar(minus_lam[:], lam_col[:], -1.0, 0.0, ALU.mult, ALU.add)
+        lam_less_one = sb.tile([P, Q_TILES], F32)
+        nc.gpsimd.tensor_scalar(lam_less_one[:], lam_col[:], 1.0, -1.0, ALU.mult, ALU.add)
+
+        reserve_or_zero = sb.tile([P, Q_TILES, 2], F32)
+        nc.gpsimd.memset(reserve_or_zero[:], 0.0)
+        nc.gpsimd.tensor_copy(reserve_or_zero[:, :, 0], reserve_col[:])
+
+        scores = []
+        for h in range(Q_TILES):
+            rows = slice(h * P, (h + 1) * P)
+            a = bank(f"score{h}", f"scores{h}")
+            nc.tensor.matmul_mx(
+                out=a[:],
+                lhsT=query_codes[:, rows].bitcast(FP8X4),
+                lhsT_scale=query_scales[:, rows],
+                rhs=key_codes[:].bitcast(FP8X4),
+                rhs_scale=key_scales[:],
+                start=True,
+                stop=True,
+            )
+            scores.append(a)
+
+        os_rows = bank("os", "os_rows")
+        for t in range(PACK):
+            nc.tensor.transpose(os_rows[:, t * P : (t + 1) * P], os_col[:, t : t + 1].to_broadcast([P, P]), identity[:])
+        fade_rows = [bank(f"fade{h}", f"fade_rows{h}") for h in range(M_BANKS)]
+        for h in range(M_BANKS):
+            for t in range(PACK):
+                nc.tensor.transpose(
+                    fade_rows[h][:, t * P : (t + 1) * P], fade_col[:, h, t : t + 1].to_broadcast([P, P]), identity[:]
+                )
+
+        picked = [sb.tile([P, I], BF16, name=f"picked{j}", tag=f"picked{j}", align_bytes=64) for j in range(E_TILES)]
+        nc.scalar.activation(picked[0][:], val_pool[0][:].indirect(slot_list[:]), ACT.Copy)
+
+        page_max = [sb.tile([P, PAGES], F32, name=f"page_max{h}") for h in range(Q_TILES)]
+        page_top = [sb.tile([P, PAGES], F32, name=f"page_top{h}") for h in range(Q_TILES)]
+        minus_max = sb.tile([P, Q_TILES], F32)
+        gapped = sb.tile([P, Q_TILES, WIDE], F32)
+        expd = sb.tile([P, Q_TILES, WIDE], F32, tag="val_pool0")
+        for h in range(Q_TILES):
+            nc.vector.tensor_reduce(page_max[h][:], scores[h][:].rearrange("p (n k) -> p n k", k=PAGE), AX.X, ALU.max)
+        for h in range(Q_TILES):
+            nc.vector.scalar_tensor_tensor(
+                gapped[:, h, 0:I].rearrange("p (n k) -> p n k", k=PAGE),
+                page_max[h][:].unsqueeze(2).to_broadcast([P, PAGES, PAGE]),
+                minus_lam[:, h : h + 1],
+                scores[h][:].rearrange("p (n k) -> p n k", k=PAGE),
+                ALU.mult,
+                ALU.add,
+            )
+            nc.vector.tensor_scalar(
+                page_top[h][:], page_max[h][:], lam_less_one[:, h : h + 1], None, ALU.mult, ALU.min,
+                accum_out=minus_max[:, h : h + 1],
+            )
+            nc.scalar.activation(
+                expd[:, h, 0:I], gapped[:, h, 0:I], ACT.Exp, bias=minus_max[:, h : h + 1], accum_out=expd[:, h, I : I + 1]
+            )
+        log_sum = sb.tile([P, Q_TILES], F32)
+        nc.scalar.activation(log_sum[:], expd[:, :, I], ACT.Ln)
+        def fade_old(j, tag):
+            product = sb.tile([P, M], F32, name=f"faded{j}", tag=tag, align_bytes=64)
+            for h in range(M_BANKS):
+                cols = slice(h * BANK, (h + 1) * BANK)
+                nc.vector.tensor_tensor(
+                    product[:, cols].rearrange("p (n t) -> p n t", t=PACK),
+                    old_sb[j][:, cols].rearrange("p (n t) -> p n t", t=PACK),
+                    fade_rows[h][:].rearrange("p (t n) -> p n t", t=PACK),
+                    ALU.mult,
+                )
+            return product
+
+        faded = [fade_old(0, "faded0"), fade_old(1, "faded1")]
+        offsets = sb.tile([P, Q_TILES, 2], F32, tag="old_sb1", align_bytes=64)
+        nc.vector.tensor_tensor(
+            offsets[:], reserve_or_zero[:], minus_max[:].unsqueeze(2).to_broadcast([P, Q_TILES, 2]), ALU.add
+        )
+        nc.vector.tensor_tensor(
+            gapped[:, :, I : I + 2], log_sum[:].unsqueeze(2).to_broadcast([P, Q_TILES, 2]), offsets[:], ALU.subtract
+        )
+        parts = [sb.tile([P, I + 1], F32, name=f"parts{h}", tag=f"parts{h}", align_bytes=64) for h in range(Q_TILES)]
+        divisor = sb.tile([P, Q_TILES], F32)
+        inverse = sb.tile([P, Q_TILES], F32)
+        for h in range(Q_TILES):
+            nc.vector.scalar_tensor_tensor(
+                parts[h][:], gapped[:, h, 0 : I + 1], gapped[:, h, I + 1 : I + 2], expd[:, h, 0 : I + 1],
+                ALU.subtract, ALU.mult, accum_out=divisor[:, h : h + 1],
+            )
+        for h in range(Q_TILES):
+            nc.vector.reciprocal(inverse[:, h : h + 1], divisor[:, h : h + 1])
+
+        weight_codes = sb.tile([P, Q], U32, align_bytes=64)
+        weight_scales = sb.tile([P, Q], U8, align_bytes=64)
+
+        def turn(slot_rows, turned, grouped, copy):
+            words = slot_rows[:].bitcast(F32)
+            for u in range(2):
+                nc.tensor.transpose(turned[:, u * P : (u + 1) * P], words[:, u : I // 2 : 2], identity[:])
+            copy(
+                grouped.bitcast(F32).rearrange("p (c u) -> p c u", u=2),
+                turned[:, 0 : 2 * P].rearrange("p (u c) -> p c u", u=2),
+            )
+
+        weights_grouped = sb.tile([P, Q * PACK], BF16, tag="weights_grouped", align_bytes=64)
+        for h in range(Q_TILES):
+            weights = sb.tile([P, I], BF16, name=f"weights{h}", align_bytes=64)
+            nc.vector.scalar_tensor_tensor(
+                weights[:].rearrange("p (n t) -> p n t", t=PACK),
+                parts[h][:, 0:I].rearrange("p (n t) -> p n t", t=PACK),
+                inverse[:, h : h + 1],
+                os_rows[:].rearrange("p (t n) -> p n t", t=PACK),
+                ALU.mult,
+                ALU.mult,
+            )
+            turn(
+                weights, bank(f"score{h}", f"weights_turned{h}"),
+                weights_grouped[:, h * P * PACK : (h + 1) * P * PACK], nc.vector.tensor_copy,
+            )
+        nc.vector.quantize_mx(out=weight_codes[:].bitcast(FP8X4), scales=weight_scales[:], in_=weights_grouped[:])
+
+        val_codes, val_scales = [], []
+        for j in range(2):
+            if j == 1:
+                nc.scalar.activation(picked[j][:], val_pool[j][:].indirect(slot_list[:]), ACT.Copy)
+            grouped = sb.tile([P, P * PACK], BF16, name=f"vals_grouped{j}", align_bytes=64)
+            turn(picked[j], bank(f"turn{j}", f"vals_turned{j}"), grouped[:], nc.scalar.copy)
+            codes = sb.tile([P, P], U32, name=f"val_codes{j}", tag=["val_codes0", "parts1"][j], align_bytes=64)
+            scales = sb.tile([P, P], U8, name=f"val_scales{j}", align_bytes=64)
+            nc.vector.quantize_mx(out=codes[:].bitcast(FP8X4), scales=scales[:], in_=grouped[:])
+            val_codes.append(codes[:])
+            val_scales.append(scales[:])
+        late_grouped = sb.tile([P, 2 * P * PACK], BF16, tag="late_grouped", align_bytes=64)
+        for j in range(2, E_TILES):
+            nc.scalar.activation(picked[j][:], val_pool[j][:].indirect(slot_list[:]), ACT.Copy)
+            turn(
+                picked[j], bank(f"turn{j % 2}", f"vals_turned{j}"),
+                late_grouped[:, (j - 2) * P * PACK : (j - 1) * P * PACK], nc.scalar.copy,
+            )
+        late_codes = sb.tile([P, 2 * P], U32, tag="weights_grouped", align_bytes=64)
+        late_scales = sb.tile([P, 2 * P], U8, align_bytes=64)
+        nc.vector.quantize_mx(out=late_codes[:].bitcast(FP8X4), scales=late_scales[:], in_=late_grouped[:])
+        for j in range(2):
+            val_codes.append(late_codes[:, j * P : (j + 1) * P])
+            val_scales.append(late_scales[:, j * P : (j + 1) * P])
+        faded.append(fade_old(2, "late_grouped"))
+        faded.append(fade_old(3, "old_sb2"))
+
+        for pair in range(2):
+            o = bank(["result", "os"][pair], f"result{pair}")
+            for k in range(2):
+                nc.tensor.matmul_mx(
+                    out=o[:, k * Q : (k + 1) * Q],
+                    lhsT=val_codes[2 * pair + k].bitcast(FP8X4),
+                    lhsT_scale=val_scales[2 * pair + k],
+                    rhs=weight_codes[:].bitcast(FP8X4),
+                    rhs_scale=weight_scales[:],
+                    start=True,
+                    stop=True,
+                )
+            o_sb = sb.tile([P, 2 * Q], F32, name=f"o_sb{pair}", tag=["picked3", "o_sb1"][pair], align_bytes=64)
+            nc.scalar.copy(o_sb[:], o[:])
+            for k in range(2):
+                j = 2 * pair + k
+                if j == 0:
+                    nc.vector.tensor_copy(placed[j][:].indirect(place_list[:]), o_sb[:, k * Q : (k + 1) * Q])
+                else:
+                    nc.scalar.activation(placed[j][:].indirect(place_list[:]), o_sb[:, k * Q : (k + 1) * Q], ACT.Copy)
+                y = sb.tile([P, M], F32, name=f"y{j}")
+                pieces = 2 if j == E_TILES - 1 else 1
+                for piece in range(pieces):
+                    cols = slice(piece * M // pieces, (piece + 1) * M // pieces)
+                    nc.vector.tensor_tensor(y[:, cols], faded[j][:, cols], placed[j][:, cols], ALU.add)
+                    nc.sync.dma_start(out[j * P : (j + 1) * P, cols], y[:, cols])

@@ -26,6 +26,8 @@ BANK = 512
 M_BANKS = M // BANK
 PAGES = I // PAGE
 WIDE = I + 8
+FADE_ROW, RESERVE_ROW = 0, 64
+VECTOR_ROWS = RESERVE_ROW + Q_TILES
 
 
 def tile_attend_pagegap_lacking_written_kernel(
@@ -42,6 +44,7 @@ def tile_attend_pagegap_lacking_written_kernel(
 
         key_scale_pool = sb.tile([P, T], U8, align_bytes=64)
 
+        vector_rows = sb.tile([P, P], F32)
         slot_list = lists.tile([P, I // 16], U16)
         nc.sync.dma_start(slot_list[:], offs)
         for quad in range(4):
@@ -53,32 +56,28 @@ def tile_attend_pagegap_lacking_written_kernel(
         nc.sync.dma_start(query_raw[:], query.rearrange("(p t) q -> p t q", t=PACK))
         key_pool = sb.tile([P, T], I32, align_bytes=64)
         nc.sync.dma_start(key_pool[:], keys_words[0].rearrange("p c t -> p (c t)").bitcast(I32))
-
         lam_col = sb.tile([P, Q_TILES], F32)
-        reserve_col = sb.tile([P, Q_TILES], F32)
-        os_col = sb.tile([P, PACK], F32)
-        fade_col = sb.tile([P, M_BANKS, PACK], F32)
-        identity = sb.tile([P, P], F32)
         with nc.allow_non_contiguous_dma(reason="one value a query row"):
             nc.sync.dma_start(lam_col[:], lam.rearrange("(h p) o -> p (h o)", p=P))
+        for first, last, vector in ((FADE_ROW, RESERVE_ROW, fade), (RESERVE_ROW, P, reserve)):
+            rows = vector.rearrange("a b -> (a b)").rearrange("(r p) -> r p", p=P)
+            nc.sync.dma_start(vector_rows[first:last, :], rows.partition_broadcast((last - first) // rows.shape[0]))
+        identity = sb.tile([P, P], F32)
         make_identity(nc, identity[:])
 
+        os_col = sb.tile([P, PACK], F32)
         val_pool = [sb.tile([P, T], F32, name=f"val_pool{j}", tag=f"val_pool{j}") for j in range(E_TILES)]
         old_sb = [sb.tile([P, M], F32, name=f"old_sb{j}", tag=f"old_sb{j}", align_bytes=64) for j in range(E_TILES)]
         place_list = lists.tile([P, Q // 16], U16)
         nc.sync.dma_start(val_pool[0][:], vals[0:P, :])
-        nc.sync.dma_start(fade_col[:], fade.rearrange("o (h p t) -> p (o h) t", p=P, t=PACK))
-        nc.sync.dma_start(old_sb[0][:], old[0:P, :])
-        nc.sync.dma_start(old_sb[1][:], old[P : 2 * P, :])
+        for j in range(E_TILES - 1):
+            nc.sync.dma_start(old_sb[j][:], old[j * P : (j + 1) * P, :])
         nc.sync.dma_start(val_pool[1][:], vals[P : 2 * P, :])
-        with nc.allow_non_contiguous_dma(reason="one value a query row"):
-            nc.sync.dma_start(reserve_col[:], reserve.rearrange("(h p) o -> p (h o)", p=P))
         nc.sync.dma_start(val_pool[2][:], vals[2 * P : 3 * P, :])
         nc.sync.dma_start(os_col[:], slot_factor.rearrange("o (p t) -> p (o t)", t=PACK))
         nc.sync.dma_start(place_list[:], offs2)
         nc.sync.dma_start(val_pool[3][:], vals[3 * P : 4 * P, :])
-        for j in range(2, E_TILES):
-            nc.sync.dma_start(old_sb[j][:], old[j * P : (j + 1) * P, :])
+        nc.sync.dma_start(old_sb[3][:], old[3 * P : 4 * P, :])
 
         placed = [sb.tile([P, M], F32, name=f"placed{j}") for j in range(E_TILES)]
         for j in range(E_TILES):
@@ -103,11 +102,6 @@ def tile_attend_pagegap_lacking_written_kernel(
         nc.gpsimd.tensor_scalar(minus_lam[:], lam_col[:], -1.0, 0.0, ALU.mult, ALU.add)
         lam_less_one = sb.tile([P, Q_TILES], F32)
         nc.gpsimd.tensor_scalar(lam_less_one[:], lam_col[:], 1.0, -1.0, ALU.mult, ALU.add)
-
-        reserve_or_zero = sb.tile([P, Q_TILES, 2], F32)
-        nc.gpsimd.memset(reserve_or_zero[:], 0.0)
-        nc.gpsimd.tensor_copy(reserve_or_zero[:, :, 0], reserve_col[:])
-
         scores = []
         for h in range(Q_TILES):
             rows = slice(h * P, (h + 1) * P)
@@ -123,21 +117,30 @@ def tile_attend_pagegap_lacking_written_kernel(
             )
             scores.append(a)
 
+        vectors_turned = bank("result0", "vectors_turned")
+        nc.tensor.transpose(vectors_turned[:, 0:P], vector_rows[:], identity[:])
+        vector_cols = sb.tile([P, VECTOR_ROWS], F32)
+        nc.scalar.copy(vector_cols[:], vectors_turned[:, 0:VECTOR_ROWS])
+        reserve_or_zero = sb.tile([P, Q_TILES, 2], F32)
+        nc.gpsimd.memset(reserve_or_zero[:], 0.0)
+        nc.gpsimd.tensor_copy(reserve_or_zero[:, :, 0], vector_cols[:, RESERVE_ROW : RESERVE_ROW + Q_TILES])
+
         os_rows = bank("os", "os_rows")
         for t in range(PACK):
             nc.tensor.transpose(os_rows[:, t * P : (t + 1) * P], os_col[:, t : t + 1].to_broadcast([P, P]), identity[:])
         fade_rows = [bank(f"fade{h}", f"fade_rows{h}") for h in range(M_BANKS)]
         for h in range(M_BANKS):
-            for t in range(PACK):
+            for t in range(BANK // P):
+                row = FADE_ROW + h * BANK // P + t
                 nc.tensor.transpose(
-                    fade_rows[h][:, t * P : (t + 1) * P], fade_col[:, h, t : t + 1].to_broadcast([P, P]), identity[:]
+                    fade_rows[h][:, t * P : (t + 1) * P], vector_cols[:, row : row + 1].to_broadcast([P, P]), identity[:]
                 )
 
         picked = [sb.tile([P, I], BF16, name=f"picked{j}", tag=f"picked{j}", align_bytes=64) for j in range(E_TILES)]
         nc.scalar.activation(picked[0][:], val_pool[0][:].indirect(slot_list[:]), ACT.Copy)
 
-        page_max = [sb.tile([P, PAGES], F32, name=f"page_max{h}") for h in range(Q_TILES)]
-        page_top = [sb.tile([P, PAGES], F32, name=f"page_top{h}") for h in range(Q_TILES)]
+        page_max = [sb.tile([P, PAGES], F32, name=f"page_max{h}", tag=f"page_max{h}", align_bytes=64) for h in range(Q_TILES)]
+        page_top = [sb.tile([P, PAGES], F32, name=f"page_top{h}", tag=f"page_top{h}", align_bytes=64) for h in range(Q_TILES)]
         minus_max = sb.tile([P, Q_TILES], F32)
         gapped = sb.tile([P, Q_TILES, WIDE], F32)
         expd = sb.tile([P, Q_TILES, WIDE], F32, tag="val_pool0")
@@ -161,19 +164,16 @@ def tile_attend_pagegap_lacking_written_kernel(
             )
         log_sum = sb.tile([P, Q_TILES], F32)
         nc.scalar.activation(log_sum[:], expd[:, :, I], ACT.Ln)
-        def fade_old(j, tag):
-            product = sb.tile([P, M], F32, name=f"faded{j}", tag=tag, align_bytes=64)
-            for h in range(M_BANKS):
-                cols = slice(h * BANK, (h + 1) * BANK)
-                nc.vector.tensor_tensor(
-                    product[:, cols].rearrange("p (n t) -> p n t", t=PACK),
-                    old_sb[j][:, cols].rearrange("p (n t) -> p n t", t=PACK),
-                    fade_rows[h][:].rearrange("p (t n) -> p n t", t=PACK),
-                    ALU.mult,
-                )
-            return product
 
-        faded = [fade_old(0, "faded0"), fade_old(1, "faded1")]
+        def fade_old(j, tag, halves):
+            scaled = sb.tile([P, BANK * len(halves)], F32, name=f"faded{j}_{halves[0]}", tag=tag, align_bytes=64)
+            for k, h in enumerate(halves):
+                nc.vector.tensor_tensor(
+                    scaled[:, k * BANK : (k + 1) * BANK], old_sb[j][:, h * BANK : (h + 1) * BANK], fade_rows[h][:], ALU.mult
+                )
+            return scaled
+
+        faded = {0: [fade_old(0, "page_max1", [0, 1])], 1: [fade_old(1, "page_top1", [0, 1])], 2: [fade_old(2, "faded2", [0])]}
         offsets = sb.tile([P, Q_TILES, 2], F32, tag="old_sb1", align_bytes=64)
         nc.vector.tensor_tensor(
             offsets[:], reserve_or_zero[:], minus_max[:].unsqueeze(2).to_broadcast([P, Q_TILES, 2]), ALU.add
@@ -206,7 +206,7 @@ def tile_attend_pagegap_lacking_written_kernel(
 
         weights_grouped = sb.tile([P, Q * PACK], BF16, tag="weights_grouped", align_bytes=64)
         for h in range(Q_TILES):
-            weights = sb.tile([P, I], BF16, name=f"weights{h}", align_bytes=64)
+            weights = sb.tile([P, I], BF16, name=f"weights{h}", tag=f"weights{h}", align_bytes=64)
             nc.vector.scalar_tensor_tensor(
                 weights[:].rearrange("p (n t) -> p n t", t=PACK),
                 parts[h][:, 0:I].rearrange("p (n t) -> p n t", t=PACK),
@@ -219,7 +219,13 @@ def tile_attend_pagegap_lacking_written_kernel(
                 weights, bank(f"score{h}", f"weights_turned{h}"),
                 weights_grouped[:, h * P * PACK : (h + 1) * P * PACK], nc.vector.tensor_copy,
             )
-        nc.vector.quantize_mx(out=weight_codes[:].bitcast(FP8X4), scales=weight_scales[:], in_=weights_grouped[:])
+            nc.vector.quantize_mx(
+                out=weight_codes[:, h * P : (h + 1) * P].bitcast(FP8X4),
+                scales=weight_scales[:, h * P : (h + 1) * P],
+                in_=weights_grouped[:, h * P * PACK : (h + 1) * P * PACK],
+            )
+
+        faded[2].append(fade_old(2, "parts0", [1]))
 
         val_codes, val_scales = [], []
         for j in range(2):
@@ -232,6 +238,7 @@ def tile_attend_pagegap_lacking_written_kernel(
             nc.vector.quantize_mx(out=codes[:].bitcast(FP8X4), scales=scales[:], in_=grouped[:])
             val_codes.append(codes[:])
             val_scales.append(scales[:])
+        faded[3] = [fade_old(3, "weights1", [0]), fade_old(3, "weights0", [1])]
         late_grouped = sb.tile([P, 2 * P * PACK], BF16, tag="late_grouped", align_bytes=64)
         for j in range(2, E_TILES):
             nc.scalar.activation(picked[j][:], val_pool[j][:].indirect(slot_list[:]), ACT.Copy)
@@ -239,38 +246,48 @@ def tile_attend_pagegap_lacking_written_kernel(
                 picked[j], bank(f"turn{j % 2}", f"vals_turned{j}"),
                 late_grouped[:, (j - 2) * P * PACK : (j - 1) * P * PACK], nc.scalar.copy,
             )
-        late_codes = sb.tile([P, 2 * P], U32, tag="weights_grouped", align_bytes=64)
+
+        def product(j, target):
+            nc.tensor.matmul_mx(
+                out=target,
+                lhsT=val_codes[j].bitcast(FP8X4),
+                lhsT_scale=val_scales[j],
+                rhs=weight_codes[:].bitcast(FP8X4),
+                rhs_scale=weight_scales[:],
+                start=True,
+                stop=True,
+            )
+
+        def add_and_store(j):
+            y = sb.tile([P, M], F32, name=f"y{j}", tag="first_sb" if j == 1 else f"y{j}", align_bytes=64)
+            width = M // len(faded[j])
+            for piece, scaled in enumerate(faded[j]):
+                cols = slice(piece * width, (piece + 1) * width)
+                nc.vector.tensor_tensor(y[:, cols], scaled[:], placed[j][:, cols], ALU.add)
+                nc.sync.dma_start(out[j * P : (j + 1) * P, cols], y[:, cols])
+
+        first_bank = bank("result0", "result0")
+        product(0, first_bank[:, 0:Q])
+        first_sb = sb.tile([P, Q], F32, tag="first_sb", align_bytes=64)
+        nc.vector.tensor_copy(first_sb[:], first_bank[:, 0:Q])
+        late_codes = sb.tile([P, 2 * P], U32, tag="val_codes0", align_bytes=64)
         late_scales = sb.tile([P, 2 * P], U8, align_bytes=64)
         nc.vector.quantize_mx(out=late_codes[:].bitcast(FP8X4), scales=late_scales[:], in_=late_grouped[:])
         for j in range(2):
             val_codes.append(late_codes[:, j * P : (j + 1) * P])
             val_scales.append(late_scales[:, j * P : (j + 1) * P])
-        faded.append(fade_old(2, "late_grouped"))
-        faded.append(fade_old(3, "old_sb2"))
-
-        for pair in range(2):
-            o = bank(["result", "os"][pair], f"result{pair}")
-            for k in range(2):
-                nc.tensor.matmul_mx(
-                    out=o[:, k * Q : (k + 1) * Q],
-                    lhsT=val_codes[2 * pair + k].bitcast(FP8X4),
-                    lhsT_scale=val_scales[2 * pair + k],
-                    rhs=weight_codes[:].bitcast(FP8X4),
-                    rhs_scale=weight_scales[:],
-                    start=True,
-                    stop=True,
-                )
-            o_sb = sb.tile([P, 2 * Q], F32, name=f"o_sb{pair}", tag=["picked3", "o_sb1"][pair], align_bytes=64)
-            nc.scalar.copy(o_sb[:], o[:])
-            for k in range(2):
-                j = 2 * pair + k
-                if j == 0:
-                    nc.vector.tensor_copy(placed[j][:].indirect(place_list[:]), o_sb[:, k * Q : (k + 1) * Q])
-                else:
-                    nc.scalar.activation(placed[j][:].indirect(place_list[:]), o_sb[:, k * Q : (k + 1) * Q], ACT.Copy)
-                y = sb.tile([P, M], F32, name=f"y{j}")
-                pieces = 2 if j == E_TILES - 1 else 1
-                for piece in range(pieces):
-                    cols = slice(piece * M // pieces, (piece + 1) * M // pieces)
-                    nc.vector.tensor_tensor(y[:, cols], faded[j][:, cols], placed[j][:, cols], ALU.add)
-                    nc.sync.dma_start(out[j * P : (j + 1) * P, cols], y[:, cols])
+        nc.vector.tensor_copy(placed[0][:].indirect(place_list[:]), first_sb[:])
+        second = bank("os", "result1")
+        product(1, second[:, 0:Q])
+        second_sb = sb.tile([P, Q], F32, tag="picked3", align_bytes=64)
+        nc.scalar.copy(second_sb[:], second[:, 0:Q])
+        nc.scalar.activation(placed[1][:].indirect(place_list[:]), second_sb[:], ACT.Copy)
+        late = bank("score0", "result23")
+        for k in range(2):
+            product(2 + k, late[:, k * Q : (k + 1) * Q])
+        late_sb = sb.tile([P, 2 * Q], F32)
+        nc.scalar.copy(late_sb[:], late[:])
+        for k in range(2):
+            nc.scalar.activation(placed[2 + k][:].indirect(place_list[:]), late_sb[:, k * Q : (k + 1) * Q], ACT.Copy)
+        for j in range(E_TILES):
+            add_and_store(j)

@@ -26,7 +26,7 @@ BANK = 512
 M_BANKS = M // BANK
 PAGES = I // PAGE
 WIDE = I + 8
-FADE_ROW, RESERVE_ROW = 0, 64
+FADE_ROW, RESERVE_ROW = 0, M // P
 VECTOR_ROWS = RESERVE_ROW + Q_TILES
 
 
@@ -42,15 +42,17 @@ def tile_attend_pagegap_lacking_written_kernel(
         def bank(tag, name):
             return ps.tile([P, BANK], F32, tag=tag, name=name)
 
-        key_scale_pool = sb.tile([P, T], U8, align_bytes=64)
+        key_scale_pool = sb.tile([P, T], U8, tag="key_scale_pool", align_bytes=64)
+        nc.gpsimd.memset(key_scale_pool[:].bitcast(I32), 0)
 
         vector_rows = sb.tile([P, P], F32)
+        nc.gpsimd.memset(vector_rows[:], 0.0)
         slot_list = lists.tile([P, I // 16], U16)
         nc.sync.dma_start(slot_list[:], offs)
         for quad in range(4):
-            nc.sync.dma_start(
-                key_scale_pool[32 * quad : 32 * quad + 32, :].bitcast(I32),
-                keys_scales[0, 4 * quad : 4 * quad + 4, :].bitcast(I32).partition_broadcast(8),
+            nc.scalar.dma_start(
+                key_scale_pool[32 * quad : 32 * quad + 4, :].bitcast(I32),
+                keys_scales[0, 4 * quad : 4 * quad + 4, :].bitcast(I32),
             )
         query_raw = sb.tile([P, PACK, Q], F32)
         nc.sync.dma_start(query_raw[:], query.rearrange("(p t) q -> p t q", t=PACK))
@@ -59,22 +61,21 @@ def tile_attend_pagegap_lacking_written_kernel(
         lam_col = sb.tile([P, Q_TILES], F32)
         with nc.allow_non_contiguous_dma(reason="one value a query row"):
             nc.sync.dma_start(lam_col[:], lam.rearrange("(h p) o -> p (h o)", p=P))
-        for first, last, vector in ((FADE_ROW, RESERVE_ROW, fade), (RESERVE_ROW, P, reserve)):
-            rows = vector.rearrange("a b -> (a b)").rearrange("(r p) -> r p", p=P)
-            nc.sync.dma_start(vector_rows[first:last, :], rows.partition_broadcast((last - first) // rows.shape[0]))
+        nc.sync.dma_start(vector_rows[FADE_ROW:RESERVE_ROW, :], fade.rearrange("o (r p) -> (o r) p", p=P))
+        nc.sync.dma_start(vector_rows[RESERVE_ROW:VECTOR_ROWS, :], reserve.rearrange("(r p) o -> r (p o)", p=P))
         identity = sb.tile([P, P], F32)
         make_identity(nc, identity[:])
 
         os_col = sb.tile([P, PACK], F32)
-        val_pool = [sb.tile([P, T], F32, name=f"val_pool{j}", tag=f"val_pool{j}") for j in range(E_TILES)]
+        val_pool = [sb.tile([P, T], F32, name=f"val_pool{j}", tag=f"val_pool{j}", align_bytes=64) for j in range(E_TILES)]
         old_sb = [sb.tile([P, M], F32, name=f"old_sb{j}", tag=f"old_sb{j}", align_bytes=64) for j in range(E_TILES)]
         place_list = lists.tile([P, Q // 16], U16)
         nc.sync.dma_start(val_pool[0][:], vals[0:P, :])
         for j in range(E_TILES - 1):
             nc.sync.dma_start(old_sb[j][:], old[j * P : (j + 1) * P, :])
         nc.sync.dma_start(val_pool[1][:], vals[P : 2 * P, :])
-        nc.sync.dma_start(val_pool[2][:], vals[2 * P : 3 * P, :])
         nc.sync.dma_start(os_col[:], slot_factor.rearrange("o (p t) -> p (o t)", t=PACK))
+        nc.sync.dma_start(val_pool[2][:], vals[2 * P : 3 * P, :])
         nc.sync.dma_start(place_list[:], offs2)
         nc.sync.dma_start(val_pool[3][:], vals[3 * P : 4 * P, :])
         nc.sync.dma_start(old_sb[3][:], old[3 * P : 4 * P, :])
@@ -95,7 +96,7 @@ def tile_attend_pagegap_lacking_written_kernel(
         nc.vector.quantize_mx(
             out=query_codes[:].bitcast(FP8X4), scales=query_scales[:], in_=query_bf[:].rearrange("p q t -> p (q t)")
         )
-        key_codes = sb.tile([P, I], U32, align_bytes=64)
+        key_codes = sb.tile([P, I], U32, tag="key_scale_pool", align_bytes=64)
         nc.vector.tensor_copy(key_codes[:], key_pool[:].bitcast(U32).indirect(slot_list[:]))
 
         minus_lam = sb.tile([P, Q_TILES], F32)
@@ -117,7 +118,7 @@ def tile_attend_pagegap_lacking_written_kernel(
             )
             scores.append(a)
 
-        vectors_turned = bank("result0", "vectors_turned")
+        vectors_turned = bank("vectors", "vectors_turned")
         nc.tensor.transpose(vectors_turned[:, 0:P], vector_rows[:], identity[:])
         vector_cols = sb.tile([P, VECTOR_ROWS], F32)
         nc.scalar.copy(vector_cols[:], vectors_turned[:, 0:VECTOR_ROWS])
@@ -143,7 +144,7 @@ def tile_attend_pagegap_lacking_written_kernel(
         page_top = [sb.tile([P, PAGES], F32, name=f"page_top{h}", tag=f"page_top{h}", align_bytes=64) for h in range(Q_TILES)]
         minus_max = sb.tile([P, Q_TILES], F32)
         gapped = sb.tile([P, Q_TILES, WIDE], F32)
-        expd = sb.tile([P, Q_TILES, WIDE], F32, tag="val_pool0")
+        expd = sb.tile([P, Q_TILES, WIDE], F32, tag="val_pool0", align_bytes=64)
         for h in range(Q_TILES):
             nc.vector.tensor_reduce(page_max[h][:], scores[h][:].rearrange("p (n k) -> p n k", k=PAGE), AX.X, ALU.max)
         for h in range(Q_TILES):
@@ -171,9 +172,9 @@ def tile_attend_pagegap_lacking_written_kernel(
                 nc.vector.tensor_tensor(
                     scaled[:, k * BANK : (k + 1) * BANK], old_sb[j][:, h * BANK : (h + 1) * BANK], fade_rows[h][:], ALU.mult
                 )
-            return scaled
+            return [scaled[:, k * BANK : (k + 1) * BANK] for k in range(len(halves))]
 
-        faded = {0: [fade_old(0, "page_max1", [0, 1])], 1: [fade_old(1, "page_top1", [0, 1])], 2: [fade_old(2, "faded2", [0])]}
+        faded = [fade_old(0, "page_max1", [0, 1]), fade_old(1, "page_top1", [0, 1]), fade_old(2, "faded2", [0])]
         offsets = sb.tile([P, Q_TILES, 2], F32, tag="old_sb1", align_bytes=64)
         nc.vector.tensor_tensor(
             offsets[:], reserve_or_zero[:], minus_max[:].unsqueeze(2).to_broadcast([P, Q_TILES, 2]), ALU.add
@@ -225,33 +226,37 @@ def tile_attend_pagegap_lacking_written_kernel(
                 in_=weights_grouped[:, h * P * PACK : (h + 1) * P * PACK],
             )
 
-        faded[2].append(fade_old(2, "parts0", [1]))
+        faded[2].extend(fade_old(2, "parts0", [1]))
 
-        val_codes, val_scales = [], []
-        for j in range(2):
-            if j == 1:
-                nc.scalar.activation(picked[j][:], val_pool[j][:].indirect(slot_list[:]), ACT.Copy)
-            grouped = sb.tile([P, P * PACK], BF16, name=f"vals_grouped{j}", align_bytes=64)
-            turn(picked[j], bank(f"turn{j}", f"vals_turned{j}"), grouped[:], nc.scalar.copy)
-            codes = sb.tile([P, P], U32, name=f"val_codes{j}", tag=["val_codes0", "parts1"][j], align_bytes=64)
-            scales = sb.tile([P, P], U8, name=f"val_scales{j}", align_bytes=64)
+        def quantise(grouped, name, tag):
+            width = grouped[:].shape[1] // PACK
+            codes = sb.tile([P, width], U32, name=f"{name}_codes", tag=tag, align_bytes=64)
+            scales = sb.tile([P, width], U8, name=f"{name}_scales", align_bytes=64)
             nc.vector.quantize_mx(out=codes[:].bitcast(FP8X4), scales=scales[:], in_=grouped[:])
-            val_codes.append(codes[:])
-            val_scales.append(scales[:])
-        faded[3] = [fade_old(3, "weights1", [0]), fade_old(3, "weights0", [1])]
-        late_grouped = sb.tile([P, 2 * P * PACK], BF16, tag="late_grouped", align_bytes=64)
-        for j in range(2, E_TILES):
+            return [(codes[:, c : c + P], scales[:, c : c + P]) for c in range(0, width, P)]
+
+        early_grouped = [sb.tile([P, P * PACK], BF16, name=f"vals_grouped{j}", align_bytes=64) for j in range(2)]
+        turn(picked[0], bank("turn0", "vals_turned0"), early_grouped[0][:], nc.scalar.copy)
+        val_operands = quantise(early_grouped[0], "vals0", "vals0_codes")
+        for j in range(1, E_TILES):
             nc.scalar.activation(picked[j][:], val_pool[j][:].indirect(slot_list[:]), ACT.Copy)
+            if j == 1:
+                turn(picked[1], bank("turn1", "vals_turned1"), early_grouped[1][:], nc.scalar.copy)
+        late_grouped = sb.tile([P, 2 * P * PACK], BF16, tag="val_pool3", align_bytes=64)
+        for j, tag in ((2, "score0"), (3, "turn1")):
             turn(
-                picked[j], bank(f"turn{j % 2}", f"vals_turned{j}"),
+                picked[j], bank(tag, f"vals_turned{j}"),
                 late_grouped[:, (j - 2) * P * PACK : (j - 1) * P * PACK], nc.scalar.copy,
             )
+        val_operands.extend(quantise(early_grouped[1], "vals1", "picked3"))
+        val_operands.extend(quantise(late_grouped, "vals23", "vals23_codes"))
+        faded.append(fade_old(3, "weights1", [0]) + fade_old(3, "weights0", [1]))
 
         def product(j, target):
             nc.tensor.matmul_mx(
                 out=target,
-                lhsT=val_codes[j].bitcast(FP8X4),
-                lhsT_scale=val_scales[j],
+                lhsT=val_operands[j][0].bitcast(FP8X4),
+                lhsT_scale=val_operands[j][1],
                 rhs=weight_codes[:].bitcast(FP8X4),
                 rhs_scale=weight_scales[:],
                 start=True,
@@ -259,30 +264,23 @@ def tile_attend_pagegap_lacking_written_kernel(
             )
 
         def add_and_store(j):
-            y = sb.tile([P, M], F32, name=f"y{j}", tag="first_sb" if j == 1 else f"y{j}", align_bytes=64)
-            width = M // len(faded[j])
-            for piece, scaled in enumerate(faded[j]):
-                cols = slice(piece * width, (piece + 1) * width)
-                nc.vector.tensor_tensor(y[:, cols], scaled[:], placed[j][:, cols], ALU.add)
+            y = sb.tile([P, M], F32, name=f"y{j}", tag="second_sb" if j == 0 else f"y{j}", align_bytes=64)
+            for h in range(M_BANKS):
+                cols = slice(h * BANK, (h + 1) * BANK)
+                nc.vector.tensor_tensor(y[:, cols], faded[j][h], placed[j][:, cols], ALU.add)
                 nc.sync.dma_start(out[j * P : (j + 1) * P, cols], y[:, cols])
 
-        first_bank = bank("result0", "result0")
+        first_bank = bank("score0", "result0")
         product(0, first_bank[:, 0:Q])
-        first_sb = sb.tile([P, Q], F32, tag="first_sb", align_bytes=64)
-        nc.vector.tensor_copy(first_sb[:], first_bank[:, 0:Q])
-        late_codes = sb.tile([P, 2 * P], U32, tag="val_codes0", align_bytes=64)
-        late_scales = sb.tile([P, 2 * P], U8, align_bytes=64)
-        nc.vector.quantize_mx(out=late_codes[:].bitcast(FP8X4), scales=late_scales[:], in_=late_grouped[:])
-        for j in range(2):
-            val_codes.append(late_codes[:, j * P : (j + 1) * P])
-            val_scales.append(late_scales[:, j * P : (j + 1) * P])
-        nc.vector.tensor_copy(placed[0][:].indirect(place_list[:]), first_sb[:])
-        second = bank("os", "result1")
-        product(1, second[:, 0:Q])
-        second_sb = sb.tile([P, Q], F32, tag="picked3", align_bytes=64)
-        nc.scalar.copy(second_sb[:], second[:, 0:Q])
-        nc.scalar.activation(placed[1][:].indirect(place_list[:]), second_sb[:], ACT.Copy)
-        late = bank("score0", "result23")
+        first_sb = sb.tile([P, Q], F32)
+        nc.scalar.copy(first_sb[:], first_bank[:, 0:Q])
+        nc.scalar.activation(placed[0][:].indirect(place_list[:]), first_sb[:], ACT.Copy)
+        second_bank = bank("os", "result1")
+        product(1, second_bank[:, 0:Q])
+        second_sb = sb.tile([P, Q], F32, tag="second_sb", align_bytes=64)
+        nc.vector.tensor_copy(second_sb[:], second_bank[:, 0:Q])
+        nc.vector.tensor_copy(placed[1][:].indirect(place_list[:]), second_sb[:])
+        late = bank("score1", "result23")
         for k in range(2):
             product(2 + k, late[:, k * Q : (k + 1) * Q])
         late_sb = sb.tile([P, 2 * Q], F32)

@@ -42,17 +42,16 @@ def tile_attend_pagegap_lacking_written_kernel(
         def bank(tag, name):
             return ps.tile([P, BANK], F32, tag=tag, name=name)
 
-        key_scale_pool = sb.tile([P, T], U8, tag="key_scale_pool", align_bytes=64)
-        nc.gpsimd.memset(key_scale_pool[:].bitcast(I32), 0)
+        key_scale_pool = sb.tile([P, T], U8, align_bytes=64)
 
         vector_rows = sb.tile([P, P], F32)
         nc.gpsimd.memset(vector_rows[:], 0.0)
         slot_list = lists.tile([P, I // 16], U16)
         nc.sync.dma_start(slot_list[:], offs)
         for quad in range(4):
-            nc.scalar.dma_start(
-                key_scale_pool[32 * quad : 32 * quad + 4, :].bitcast(I32),
-                keys_scales[0, 4 * quad : 4 * quad + 4, :].bitcast(I32),
+            nc.sync.dma_start(
+                key_scale_pool[32 * quad : 32 * quad + 32, :].bitcast(I32),
+                keys_scales[0, 4 * quad : 4 * quad + 4, :].bitcast(I32).partition_broadcast(8),
             )
         query_raw = sb.tile([P, PACK, Q], F32)
         nc.sync.dma_start(query_raw[:], query.rearrange("(p t) q -> p t q", t=PACK))
@@ -96,7 +95,7 @@ def tile_attend_pagegap_lacking_written_kernel(
         nc.vector.quantize_mx(
             out=query_codes[:].bitcast(FP8X4), scales=query_scales[:], in_=query_bf[:].rearrange("p q t -> p (q t)")
         )
-        key_codes = sb.tile([P, I], U32, tag="key_scale_pool", align_bytes=64)
+        key_codes = sb.tile([P, I], U32, align_bytes=64)
         nc.vector.tensor_copy(key_codes[:], key_pool[:].bitcast(U32).indirect(slot_list[:]))
 
         minus_lam = sb.tile([P, Q_TILES], F32)

from contextlib import ExitStack

import concourse.mybir as mybir
from concourse.masks import make_identity

D, T, I, Q, E, M = 512, 2048, 512, 256, 512, 1024
PAGE = 8
P = 128
PACK = 4
FLOPS = 2 * D * Q * I + 2 * I * E * Q

F32 = mybir.dt.float32
BF16 = mybir.dt.bfloat16
I32 = mybir.dt.int32
U32 = mybir.dt.uint32
U16 = mybir.dt.uint16
U8 = mybir.dt.uint8
FP8X4 = mybir.dt.float8_e4m3fn_x4
ALU = mybir.AluOpType
ACT = mybir.ActivationFunctionType
AX = mybir.AxisListType

Q_TILES = Q // P
E_TILES = E // P
BANK = 512
M_BANKS = M // BANK
PAGES = I // PAGE
WIDE = I + 8
FADE_ROW, RESERVE_ROW = 0, M // P
VECTOR_ROWS = RESERVE_ROW + Q_TILES


def tile_attend_pagegap_lacking_written_kernel(
    tc, query, keys_words, keys_scales, lam, reserve, slot_factor, vals, old, fade, offs, offs2, out
):
    nc = tc.nc
    with ExitStack() as ctx:
        lists = ctx.enter_context(tc.tile_pool(name="lists", bufs=1))
        sb = ctx.enter_context(tc.tile_pool(name="sb", bufs=1))
        ps = ctx.enter_context(tc.psum_pool(name="ps", bufs=1))

        def bank(tag, name):
            return ps.tile([P, BANK], F32, tag=tag, name=name)

        key_scale_pool = sb.tile([P, T], U8, align_bytes=64)

        vector_rows = sb.tile([P, P], F32)
        nc.gpsimd.memset(vector_rows[:], 0.0)
        slot_list = lists.tile([P, I // 16], U16)
        nc.sync.dma_start(slot_list[:], offs)
        for quad in range(4):
            nc.sync.dma_start(
                key_scale_pool[32 * quad : 32 * quad + 32, :].bitcast(I32),
                keys_scales[0, 4 * quad : 4 * quad + 4, :].bitcast(I32).partition_broadcast(8),
            )
        query_raw = sb.tile([P, PACK, Q], F32)
        nc.sync.dma_start(query_raw[:], query.rearrange("(p t) q -> p t q", t=PACK))
        key_pool = sb.tile([P, T], I32, align_bytes=64)
        nc.sync.dma_start(key_pool[:], keys_words[0].rearrange("p c t -> p (c t)").bitcast(I32))
        lam_col = sb.tile([P, Q_TILES], F32)
        with nc.allow_non_contiguous_dma(reason="one value a query row"):
            nc.sync.dma_start(lam_col[:], lam.rearrange("(h p) o -> p (h o)", p=P))
        nc.sync.dma_start(vector_rows[FADE_ROW:RESERVE_ROW, :], fade.rearrange("o (r p) -> (o r) p", p=P))
        nc.sync.dma_start(vector_rows[RESERVE_ROW:VECTOR_ROWS, :], reserve.rearrange("(r p) o -> r (p o)", p=P))
        identity = sb.tile([P, P], F32)
        make_identity(nc, identity[:])

        os_col = sb.tile([P, PACK], F32)
        val_pool = [sb.tile([P, T], F32, name=f"val_pool{j}", tag=f"val_pool{j}", align_bytes=64) for j in range(E_TILES)]
        old_sb = [sb.tile([P, M], F32, name=f"old_sb{j}", tag=f"old_sb{j}", align_bytes=64) for j in range(E_TILES)]
        place_list = lists.tile([P, Q // 16], U16)
        nc.sync.dma_start(val_pool[0][:], vals[0:P, :])
        for j in range(E_TILES - 1):
            nc.sync.dma_start(old_sb[j][:], old[j * P : (j + 1) * P, :])
        nc.sync.dma_start(val_pool[1][:], vals[P : 2 * P, :])
        nc.sync.dma_start(os_col[:], slot_factor.rearrange("o (p t) -> p (o t)", t=PACK))
        nc.sync.dma_start(val_pool[2][:], vals[2 * P : 3 * P, :])
        nc.sync.dma_start(place_list[:], offs2)
        nc.sync.dma_start(val_pool[3][:], vals[3 * P : 4 * P, :])
        nc.sync.dma_start(old_sb[3][:], old[3 * P : 4 * P, :])

        placed = [sb.tile([P, M], F32, name=f"placed{j}") for j in range(E_TILES)]
        for j in range(E_TILES):
            nc.vector.memset(placed[j][:], 0.0)

        key_scales = sb.tile([P, I], U8, align_bytes=64)
        nc.vector.tensor_copy(key_scales[:], key_scale_pool[:].indirect(slot_list[:]))
        query_bf = sb.tile([P, Q, PACK], BF16, align_bytes=64)
        nc.scalar.copy(
            query_bf[:].rearrange("p (c n) t -> p c t n", n=4),
            query_raw[:].rearrange("p t (c n) -> p c t n", n=4),
        )
        query_codes = sb.tile([P, Q], U32, align_bytes=64)
        query_scales = sb.tile([P, Q], U8, align_bytes=64)
        nc.vector.quantize_mx(
            out=query_codes[:].bitcast(FP8X4), scales=query_scales[:], in_=query_bf[:].rearrange("p q t -> p (q t)")
        )
        key_codes = sb.tile([P, I], U32, align_bytes=64)
        nc.vector.tensor_copy(key_codes[:], key_pool[:].bitcast(U32).indirect(slot_list[:]))

        minus_lam = sb.tile([P, Q_TILES], F32)
        nc.gpsimd.tensor_scalar(minus_lam[:], lam_col[:], -1.0, 0.0, ALU.mult, ALU.add)
        lam_less_one = sb.tile([P, Q_TILES], F32)
        nc.gpsimd.tensor_scalar(lam_less_one[:], lam_col[:], 1.0, -1.0, ALU.mult, ALU.add)
        scores = []
        for h in range(Q_TILES):
            rows = slice(h * P, (h + 1) * P)
            a = bank(f"score{h}", f"scores{h}")
            nc.tensor.matmul_mx(
                out=a[:],
                lhsT=query_codes[:, rows].bitcast(FP8X4),
                lhsT_scale=query_scales[:, rows],
                rhs=key_codes[:].bitcast(FP8X4),
                rhs_scale=key_scales[:],
                start=True,
                stop=True,
            )
            scores.append(a)

        vectors_turned = bank("vectors", "vectors_turned")
        nc.tensor.transpose(vectors_turned[:, 0:P], vector_rows[:], identity[:])
        vector_cols = sb.tile([P, VECTOR_ROWS], F32)
        nc.scalar.copy(vector_cols[:], vectors_turned[:, 0:VECTOR_ROWS])
        reserve_or_zero = sb.tile([P, Q_TILES, 2], F32)
        nc.gpsimd.memset(reserve_or_zero[:], 0.0)
        nc.gpsimd.tensor_copy(reserve_or_zero[:, :, 0], vector_cols[:, RESERVE_ROW : RESERVE_ROW + Q_TILES])

        os_rows = bank("os", "os_rows")
        for t in range(PACK):
            nc.tensor.transpose(os_rows[:, t * P : (t + 1) * P], os_col[:, t : t + 1].to_broadcast([P, P]), identity[:])
        fade_rows = [bank(f"fade{h}", f"fade_rows{h}") for h in range(M_BANKS)]
        for h in range(M_BANKS):
            for t in range(BANK // P):
                row = FADE_ROW + h * BANK // P + t
                nc.tensor.transpose(
                    fade_rows[h][:, t * P : (t + 1) * P], vector_cols[:, row : row + 1].to_broadcast([P, P]), identity[:]
                )

        picked = [sb.tile([P, I], BF16, name=f"picked{j}", tag=f"picked{j}", align_bytes=64) for j in range(E_TILES)]
        nc.scalar.activation(picked[0][:], val_pool[0][:].indirect(slot_list[:]), ACT.Copy)

        page_max = [sb.tile([P, PAGES], F32, name=f"page_max{h}", tag=f"page_max{h}", align_bytes=64) for h in range(Q_TILES)]
        page_top = [sb.tile([P, PAGES], F32, name=f"page_top{h}", tag=f"page_top{h}", align_bytes=64) for h in range(Q_TILES)]
        minus_max = sb.tile([P, Q_TILES], F32)
        gapped = sb.tile([P, Q_TILES, WIDE], F32)
        expd = sb.tile([P, Q_TILES, WIDE], F32, tag="val_pool0", align_bytes=64)
        for h in range(Q_TILES):
            nc.vector.tensor_reduce(page_max[h][:], scores[h][:].rearrange("p (n k) -> p n k", k=PAGE), AX.X, ALU.max)
        for h in range(Q_TILES):
            nc.vector.scalar_tensor_tensor(
                gapped[:, h, 0:I].rearrange("p (n k) -> p n k", k=PAGE),
                page_max[h][:].unsqueeze(2).to_broadcast([P, PAGES, PAGE]),
                minus_lam[:, h : h + 1],
                scores[h][:].rearrange("p (n k) -> p n k", k=PAGE),
                ALU.mult,
                ALU.add,
            )
            nc.vector.tensor_scalar(
                page_top[h][:], page_max[h][:], lam_less_one[:, h : h + 1], None, ALU.mult, ALU.min,
                accum_out=minus_max[:, h : h + 1],
            )
            nc.scalar.activation(
                expd[:, h, 0:I], gapped[:, h, 0:I], ACT.Exp, bias=minus_max[:, h : h + 1], accum_out=expd[:, h, I : I + 1]
            )
        log_sum = sb.tile([P, Q_TILES], F32)
        nc.scalar.activation(log_sum[:], expd[:, :, I], ACT.Ln)

        def fade_old(j, tag, halves):
            scaled = sb.tile([P, BANK * len(halves)], F32, name=f"faded{j}_{halves[0]}", tag=tag, align_bytes=64)
            for k, h in enumerate(halves):
                nc.vector.tensor_tensor(
                    scaled[:, k * BANK : (k + 1) * BANK], old_sb[j][:, h * BANK : (h + 1) * BANK], fade_rows[h][:], ALU.mult
                )
            return [scaled[:, k * BANK : (k + 1) * BANK] for k in range(len(halves))]

        faded = [fade_old(0, "page_max1", [0, 1]), fade_old(1, "page_top1", [0, 1]), fade_old(2, "faded2", [0])]
        offsets = sb.tile([P, Q_TILES, 2], F32, tag="old_sb1", align_bytes=64)
        nc.vector.tensor_tensor(
            offsets[:], reserve_or_zero[:], minus_max[:].unsqueeze(2).to_broadcast([P, Q_TILES, 2]), ALU.add
        )
        nc.vector.tensor_tensor(
            gapped[:, :, I : I + 2], log_sum[:].unsqueeze(2).to_broadcast([P, Q_TILES, 2]), offsets[:], ALU.subtract
        )
        parts = [sb.tile([P, I + 1], F32, name=f"parts{h}", tag=f"parts{h}", align_bytes=64) for h in range(Q_TILES)]
        divisor = sb.tile([P, Q_TILES], F32)
        inverse = sb.tile([P, Q_TILES], F32)
        for h in range(Q_TILES):
            nc.vector.scalar_tensor_tensor(
                parts[h][:], gapped[:, h, 0 : I + 1], gapped[:, h, I + 1 : I + 2], expd[:, h, 0 : I + 1],
                ALU.subtract, ALU.mult, accum_out=divisor[:, h : h + 1],
            )
        for h in range(Q_TILES):
            nc.vector.reciprocal(inverse[:, h : h + 1], divisor[:, h : h + 1])

        weight_codes = sb.tile([P, Q], U32, align_bytes=64)
        weight_scales = sb.tile([P, Q], U8, align_bytes=64)

        def turn(slot_rows, turned, grouped, copy):
            words = slot_rows[:].bitcast(F32)
            for u in range(2):
                nc.tensor.transpose(turned[:, u * P : (u + 1) * P], words[:, u : I // 2 : 2], identity[:])
            copy(
                grouped.bitcast(F32).rearrange("p (c u) -> p c u", u=2),
                turned[:, 0 : 2 * P].rearrange("p (u c) -> p c u", u=2),
            )

        weights_grouped = sb.tile([P, Q * PACK], BF16, tag="weights_grouped", align_bytes=64)
        for h in range(Q_TILES):
            weights = sb.tile([P, I], BF16, name=f"weights{h}", tag=f"weights{h}", align_bytes=64)
            nc.vector.scalar_tensor_tensor(
                weights[:].rearrange("p (n t) -> p n t", t=PACK),
                parts[h][:, 0:I].rearrange("p (n t) -> p n t", t=PACK),
                inverse[:, h : h + 1],
                os_rows[:].rearrange("p (t n) -> p n t", t=PACK),
                ALU.mult,
                ALU.mult,
            )
            turn(
                weights, bank(f"score{h}", f"weights_turned{h}"),
                weights_grouped[:, h * P * PACK : (h + 1) * P * PACK], nc.vector.tensor_copy,
            )
            nc.vector.quantize_mx(
                out=weight_codes[:, h * P : (h + 1) * P].bitcast(FP8X4),
                scales=weight_scales[:, h * P : (h + 1) * P],
                in_=weights_grouped[:, h * P * PACK : (h + 1) * P * PACK],
            )

        faded[2].extend(fade_old(2, "parts0", [1]))

        def quantise(grouped, name, tag):
            width = grouped[:].shape[1] // PACK
            codes = sb.tile([P, width], U32, name=f"{name}_codes", tag=tag, align_bytes=64)
            scales = sb.tile([P, width], U8, name=f"{name}_scales", align_bytes=64)
            nc.vector.quantize_mx(out=codes[:].bitcast(FP8X4), scales=scales[:], in_=grouped[:])
            return [(codes[:, c : c + P], scales[:, c : c + P]) for c in range(0, width, P)]

        early_grouped = [sb.tile([P, P * PACK], BF16, name=f"vals_grouped{j}", align_bytes=64) for j in range(2)]
        turn(picked[0], bank("turn0", "vals_turned0"), early_grouped[0][:], nc.scalar.copy)
        val_operands = quantise(early_grouped[0], "vals0", "vals0_codes")
        for j in range(1, E_TILES):
            nc.scalar.activation(picked[j][:], val_pool[j][:].indirect(slot_list[:]), ACT.Copy)
            if j == 1:
                turn(picked[1], bank("turn1", "vals_turned1"), early_grouped[1][:], nc.scalar.copy)
        late_grouped = sb.tile([P, 2 * P * PACK], BF16, tag="val_pool3", align_bytes=64)
        for j, tag in ((2, "score0"), (3, "turn1")):
            turn(
                picked[j], bank(tag, f"vals_turned{j}"),
                late_grouped[:, (j - 2) * P * PACK : (j - 1) * P * PACK], nc.scalar.copy,
            )
        val_operands.extend(quantise(early_grouped[1], "vals1", "picked3"))
        val_operands.extend(quantise(late_grouped, "vals23", "vals23_codes"))
        faded.append(fade_old(3, "weights1", [0]) + fade_old(3, "weights0", [1]))

        def product(j, target):
            nc.tensor.matmul_mx(
                out=target,
                lhsT=val_operands[j][0].bitcast(FP8X4),
                lhsT_scale=val_operands[j][1],
                rhs=weight_codes[:].bitcast(FP8X4),
                rhs_scale=weight_scales[:],
                start=True,
                stop=True,
            )

        def add_and_store(j):
            y = sb.tile([P, M], F32, name=f"y{j}", tag="second_sb" if j == 0 else f"y{j}", align_bytes=64)
            for h in range(M_BANKS):
                cols = slice(h * BANK, (h + 1) * BANK)
                nc.vector.tensor_tensor(y[:, cols], faded[j][h], placed[j][:, cols], ALU.add)
                nc.sync.dma_start(out[j * P : (j + 1) * P, cols], y[:, cols])

        first_bank = bank("score0", "result0")
        product(0, first_bank[:, 0:Q])
        first_sb = sb.tile([P, Q], F32)
        nc.scalar.copy(first_sb[:], first_bank[:, 0:Q])
        nc.scalar.activation(placed[0][:].indirect(place_list[:]), first_sb[:], ACT.Copy)
        second_bank = bank("os", "result1")
        product(1, second_bank[:, 0:Q])
        second_sb = sb.tile([P, Q], F32, tag="second_sb", align_bytes=64)
        nc.vector.tensor_copy(second_sb[:], second_bank[:, 0:Q])
        nc.vector.tensor_copy(placed[1][:].indirect(place_list[:]), second_sb[:])
        late = bank("score1", "result23")
        for k in range(2):
            product(2 + k, late[:, k * Q : (k + 1) * Q])
        late_sb = sb.tile([P, 2 * Q], F32)
        nc.scalar.copy(late_sb[:], late[:])
        for k in range(2):
            nc.scalar.activation(placed[2 + k][:].indirect(place_list[:]), late_sb[:, k * Q : (k + 1) * Q], ACT.Copy)
        for j in range(E_TILES):
            add_and_store(j)
